import numpy as np
import ml_dtypes

BF16 = ml_dtypes.bfloat16


def bf(x):
    return np.asarray(x, np.float32).astype(BF16)


def f32(x):
    return np.asarray(x, np.float32)


def f64(x):
    return np.asarray(x).astype(np.float64)


def striped(idx):
    return np.tile(idx.reshape(-1, 16).T, (8, 1))


S, K, M, N, E, Q = 512, 512, 512, 256, 1, 256


def setup_inputs():
    return {"base": bf(np.random.standard_normal((M, S))), "x": bf(np.random.standard_normal((K, N))), "w": bf(1.2 * np.random.standard_normal((E, K, M)) / np.sqrt(K)), "s": f32(0.5 + np.random.random_sample((M, 1))), "offs": striped(np.random.permutation(S)[:N])}


def reference(base, x, w, s, offs):
    idx = offs[:16].T.reshape(-1)
    z = f64(base).copy()
    for e in range(E):
        z[:, idx[e * Q : (e + 1) * Q]] += f64(w)[e].T @ f64(x)[:, e * Q : (e + 1) * Q]
    z = z / np.sqrt((z**2).mean(axis=0, keepdims=True) + 1e-5) * f64(s)
    return z

@@ -1,0 +1,72 @@
+import concourse.mybir as mybir
+from concourse.masks import make_identity
+
+BF16, F32, U16 = mybir.dt.bfloat16, mybir.dt.float32, mybir.dt.uint16
+Act = mybir.ActivationFunctionType
+mult = mybir.AluOpType.mult
+
+P = 128
+TOKENS = 512
+FEATURES = 512
+CONTRACTION = 512
+LIST = 256
+EPS = 1e-5
+WINDOWS = FEATURES // P
+BLOCKS = CONTRACTION // P
+
+FLOPS = 2 * CONTRACTION * FEATURES * LIST
+
+
+def tile_rows_placenorm_base_kernel(tc, base, x, w, s, offs, out):
+    nc = tc.nc
+    with (
+        tc.tile_pool(name="held", bufs=1) as held,
+        tc.tile_pool(name="squares", bufs=WINDOWS) as squares,
+        tc.tile_pool(name="results", bufs=WINDOWS) as results,
+        tc.psum_pool(name="psum", bufs=1) as psum,
+    ):
+        base_tile = held.tile([P, WINDOWS, TOKENS], BF16)
+        nc.sync.dma_start(base_tile[:], base.rearrange("(a p) i -> p a i", p=P))
+        offsets = held.tile([P, LIST // 16], U16)
+        nc.sync.dma_start(offsets[:], offs)
+        x_tile = held.tile([P, BLOCKS, LIST], BF16)
+        nc.sync.dma_start(x_tile[:], x.rearrange("(p k) j -> p k j", p=P))
+        w_tile = held.tile([P, BLOCKS, FEATURES], BF16)
+        nc.sync.dma_start(w_tile[:], w.flatten_outer_dims().rearrange("(p k) m -> p k m", p=P))
+        gain = held.tile([P, WINDOWS], F32)
+        nc.sync.dma_start(gain[:], s.rearrange("(a p) o -> p (a o)", p=P))
+
+        ident = held.tile([P, P], BF16)
+        make_identity(nc, ident[:])
+        mean_weights = held.tile([P, P], BF16)
+        nc.vector.memset(mean_weights[:], 1.0 / FEATURES)
+        eps = held.tile([P, 1], F32)
+        nc.vector.memset(eps[:], EPS)
+
+        windows = [psum.tile([P, TOKENS], F32, name=f"window{a}") for a in range(WINDOWS)]
+        for a in range(WINDOWS):
+            nc.tensor.matmul(windows[a][:], ident[:], base_tile[:, a, :], start=True, stop=False)
+
+        for a in range(WINDOWS):
+            for k in range(BLOCKS):
+                nc.tensor.matmul(
+                    windows[a][:].indirect(offsets[:]),
+                    w_tile[:, k, a * P : (a + 1) * P],
+                    x_tile[:, k, :],
+                    start=False,
+                    stop=k == BLOCKS - 1,
+                )
+
+        squared = [squares.tile([P, TOKENS], BF16, name="squared") for a in range(WINDOWS)]
+        mean = psum.tile([P, TOKENS], F32)
+        for a in range(WINDOWS):
+            nc.scalar.activation(squared[a][:], windows[a][:], Act.Square)
+        for a in range(WINDOWS):
+            nc.tensor.matmul(mean[:], mean_weights[:], squared[a][:], start=a == 0, stop=a == WINDOWS - 1)
+        rstd = held.tile([P, TOKENS], F32)
+        nc.scalar.activation(rstd[:], mean[:], Act.Abs_reciprocal_sqrt, bias=eps[:])
+
+        for a in range(WINDOWS):
+            result = results.tile([P, TOKENS], F32)
+            nc.vector.scalar_tensor_tensor(result[:], windows[a][:], gain[:, a : a + 1], rstd[:], mult, mult)
+            nc.sync.dma_start(out[a * P : (a + 1) * P, :], result[:])

@@ -11,6 +11,8 @@ FEATURES = 512
 CONTRACTION = 512
 LIST = 256
 EPS = 1e-5
+HALF = TOKENS // 2
+WARM_UPS = 4
 WINDOWS = FEATURES // P
 BLOCKS = CONTRACTION // P
 
@@ -22,9 +24,19 @@ def tile_rows_placenorm_base_kernel(tc, base, x, w, s, offs, out):
     with (
         tc.tile_pool(name="held", bufs=1) as held,
         tc.tile_pool(name="squares", bufs=WINDOWS) as squares,
-        tc.tile_pool(name="results", bufs=WINDOWS) as results,
+        tc.tile_pool(name="results", bufs=2 * WINDOWS) as results,
         tc.psum_pool(name="psum", bufs=1) as psum,
     ):
+        zeros = held.tile([P, TOKENS], BF16)
+        nc.vector.memset(zeros[:], 0.0)
+        unread = psum.tile([P, TOKENS], F32)
+        for i in range(WARM_UPS):
+            nc.tensor.matmul(unread[:], zeros[:, :P], zeros[:], start=True, stop=True)
+        eps = held.tile([P, 1], F32)
+        nc.vector.memset(eps[:], EPS)
+        unread_rstd = held.tile([P, 1], F32)
+        nc.scalar.activation(unread_rstd[:], eps[:], Act.Abs_reciprocal_sqrt, bias=eps[:])
+
         base_tile = held.tile([P, WINDOWS, TOKENS], BF16)
         nc.sync.dma_start(base_tile[:], base.rearrange("(a p) i -> p a i", p=P))
         offsets = held.tile([P, LIST // 16], U16)
@@ -40,8 +52,6 @@ def tile_rows_placenorm_base_kernel(tc, base, x, w, s, offs, out):
         make_identity(nc, ident[:])
         mean_weights = held.tile([P, P], BF16)
         nc.vector.memset(mean_weights[:], 1.0 / FEATURES)
-        eps = held.tile([P, 1], F32)
-        nc.vector.memset(eps[:], EPS)
 
         windows = [psum.tile([P, TOKENS], F32, name=f"window{a}") for a in range(WINDOWS)]
         for a in range(WINDOWS):
@@ -57,16 +67,25 @@ def tile_rows_placenorm_base_kernel(tc, base, x, w, s, offs, out):
                     stop=k == BLOCKS - 1,
                 )
 
+        halves = [slice(h * HALF, (h + 1) * HALF) for h in range(2)]
         squared = [squares.tile([P, TOKENS], BF16, name="squared") for a in range(WINDOWS)]
-        mean = psum.tile([P, TOKENS], F32)
-        for a in range(WINDOWS):
+        for a in range(WINDOWS - 1):
             nc.scalar.activation(squared[a][:], windows[a][:], Act.Square)
+        for half in halves:
+            nc.scalar.activation(squared[-1][:, half], windows[-1][:, half], Act.Square)
+        means = [psum.tile([P, HALF], F32, name=f"mean{h}") for h in range(2)]
         for a in range(WINDOWS):
-            nc.tensor.matmul(mean[:], mean_weights[:], squared[a][:], start=a == 0, stop=a == WINDOWS - 1)
-        rstd = held.tile([P, TOKENS], F32)
-        nc.scalar.activation(rstd[:], mean[:], Act.Abs_reciprocal_sqrt, bias=eps[:])
+            for h in range(2):
+                nc.tensor.matmul(
+                    means[h][:], mean_weights[:], squared[a][:, halves[h]], start=a == 0, stop=a == WINDOWS - 1
+                )
 
-        for a in range(WINDOWS):
-            result = results.tile([P, TOKENS], F32)
-            nc.vector.scalar_tensor_tensor(result[:], windows[a][:], gain[:, a : a + 1], rstd[:], mult, mult)
-            nc.sync.dma_start(out[a * P : (a + 1) * P, :], result[:])
+        for h in range(2):
+            rstd = results.tile([P, HALF], F32)
+            nc.scalar.activation(rstd[:], means[h][:], Act.Abs_reciprocal_sqrt, bias=eps[:])
+            for a in range(WINDOWS):
+                result = results.tile([P, HALF], F32)
+                nc.vector.scalar_tensor_tensor(
+                    result[:], windows[a][:, halves[h]], gain[:, a : a + 1], rstd[:], mult, mult
+                )
+                nc.sync.dma_start(out[a * P : (a + 1) * P, halves[h]], result[:])

@@ -12,7 +12,7 @@ CONTRACTION = 512
 LIST = 256
 EPS = 1e-5
 HALF = TOKENS // 2
-WARM_UPS = 4
+WARM_UPS = 3
 WINDOWS = FEATURES // P
 BLOCKS = CONTRACTION // P
 
@@ -38,13 +38,17 @@ def tile_rows_placenorm_base_kernel(tc, base, x, w, s, offs, out):
         nc.scalar.activation(unread_rstd[:], eps[:], Act.Abs_reciprocal_sqrt, bias=eps[:])
 
         base_tile = held.tile([P, WINDOWS, TOKENS], BF16)
-        nc.sync.dma_start(base_tile[:], base.rearrange("(a p) i -> p a i", p=P))
+        base_blocks = base.rearrange("(a p) i -> p a i", p=P)
+        for a in range(0, WINDOWS, 2):
+            nc.sync.dma_start(base_tile[:, a : a + 2, :], base_blocks[:, a : a + 2, :])
         offsets = held.tile([P, LIST // 16], U16)
         nc.sync.dma_start(offsets[:], offs)
         x_tile = held.tile([P, BLOCKS, LIST], BF16)
         nc.sync.dma_start(x_tile[:], x.rearrange("(p k) j -> p k j", p=P))
         w_tile = held.tile([P, BLOCKS, FEATURES], BF16)
-        nc.sync.dma_start(w_tile[:], w.flatten_outer_dims().rearrange("(p k) m -> p k m", p=P))
+        w_blocks = w.flatten_outer_dims().rearrange("(p k) m -> p k m", p=P)
+        for k in range(0, BLOCKS, 2):
+            nc.sync.dma_start(w_tile[:, k : k + 2, :], w_blocks[:, k : k + 2, :])
         gain = held.tile([P, WINDOWS], F32)
         nc.sync.dma_start(gain[:], s.rearrange("(a p) o -> p (a o)", p=P))
 
@@ -57,15 +61,16 @@ def tile_rows_placenorm_base_kernel(tc, base, x, w, s, offs, out):
         for a in range(WINDOWS):
             nc.tensor.matmul(windows[a][:], ident[:], base_tile[:, a, :], start=True, stop=False)
 
-        for a in range(WINDOWS):
-            for k in range(BLOCKS):
-                nc.tensor.matmul(
-                    windows[a][:].indirect(offsets[:]),
-                    w_tile[:, k, a * P : (a + 1) * P],
-                    x_tile[:, k, :],
-                    start=False,
-                    stop=k == BLOCKS - 1,
-                )
+        for k_half in range(0, BLOCKS, 2):
+            for a in range(WINDOWS):
+                for k in range(k_half, k_half + 2):
+                    nc.tensor.matmul(
+                        windows[a][:].indirect(offsets[:]),
+                        w_tile[:, k, a * P : (a + 1) * P],
+                        x_tile[:, k, :],
+                        start=False,
+                        stop=k == BLOCKS - 1,
+                    )
 
         halves = [slice(h * HALF, (h + 1) * HALF) for h in range(2)]
         squared = [squares.tile([P, TOKENS], BF16, name="squared") for a in range(WINDOWS)]
@@ -74,8 +79,8 @@ def tile_rows_placenorm_base_kernel(tc, base, x, w, s, offs, out):
         for half in halves:
             nc.scalar.activation(squared[-1][:, half], windows[-1][:, half], Act.Square)
         means = [psum.tile([P, HALF], F32, name=f"mean{h}") for h in range(2)]
-        for a in range(WINDOWS):
-            for h in range(2):
+        for h in range(2):
+            for a in range(WINDOWS):
                 nc.tensor.matmul(
                     means[h][:], mean_weights[:], squared[a][:, halves[h]], start=a == 0, stop=a == WINDOWS - 1
                 )

@@ -44,11 +44,14 @@ def tile_rows_placenorm_base_kernel(tc, base, x, w, s, offs, out):
         offsets = held.tile([P, LIST // 16], U16)
         nc.sync.dma_start(offsets[:], offs)
         x_tile = held.tile([P, BLOCKS, LIST], BF16)
-        nc.sync.dma_start(x_tile[:], x.rearrange("(p k) j -> p k j", p=P))
         w_tile = held.tile([P, BLOCKS, FEATURES], BF16)
+        x_blocks = x.rearrange("(p k) j -> p k j", p=P)
         w_blocks = w.flatten_outer_dims().rearrange("(p k) m -> p k m", p=P)
-        for k in range(0, BLOCKS, 2):
-            nc.sync.dma_start(w_tile[:, k : k + 2, :], w_blocks[:, k : k + 2, :])
+        nc.sync.dma_start(x_tile[:, 0:2, :], x_blocks[:, 0:2, :])
+        nc.sync.dma_start(w_tile[:, 0:1, :], w_blocks[:, 0:1, :])
+        nc.sync.dma_start(w_tile[:, 1:2, :], w_blocks[:, 1:2, :])
+        nc.sync.dma_start(x_tile[:, 2:4, :], x_blocks[:, 2:4, :])
+        nc.sync.dma_start(w_tile[:, 2:4, :], w_blocks[:, 2:4, :])
         gain = held.tile([P, WINDOWS], F32)
         nc.sync.dma_start(gain[:], s.rearrange("(a p) o -> p (a o)", p=P))
 
@@ -61,9 +64,9 @@ def tile_rows_placenorm_base_kernel(tc, base, x, w, s, offs, out):
         for a in range(WINDOWS):
             nc.tensor.matmul(windows[a][:], ident[:], base_tile[:, a, :], start=True, stop=False)
 
-        for k_half in range(0, BLOCKS, 2):
+        for blocks in ((0,), (1,), (2, 3)):
             for a in range(WINDOWS):
-                for k in range(k_half, k_half + 2):
+                for k in blocks:
                     nc.tensor.matmul(
                         windows[a][:].indirect(offsets[:]),
                         w_tile[:, k, a * P : (a + 1) * P],

import concourse.mybir as mybir
from concourse.masks import make_identity

BF16, F32, U16 = mybir.dt.bfloat16, mybir.dt.float32, mybir.dt.uint16
Act = mybir.ActivationFunctionType
mult = mybir.AluOpType.mult

P = 128
TOKENS = 512
FEATURES = 512
CONTRACTION = 512
LIST = 256
EPS = 1e-5
HALF = TOKENS // 2
WARM_UPS = 3
WINDOWS = FEATURES // P
BLOCKS = CONTRACTION // P

FLOPS = 2 * CONTRACTION * FEATURES * LIST


def tile_rows_placenorm_base_kernel(tc, base, x, w, s, offs, out):
    nc = tc.nc
    with (
        tc.tile_pool(name="held", bufs=1) as held,
        tc.tile_pool(name="squares", bufs=WINDOWS) as squares,
        tc.tile_pool(name="results", bufs=2 * WINDOWS) as results,
        tc.psum_pool(name="psum", bufs=1) as psum,
    ):
        zeros = held.tile([P, TOKENS], BF16)
        nc.vector.memset(zeros[:], 0.0)
        unread = psum.tile([P, TOKENS], F32)
        for i in range(WARM_UPS):
            nc.tensor.matmul(unread[:], zeros[:, :P], zeros[:], start=True, stop=True)
        eps = held.tile([P, 1], F32)
        nc.vector.memset(eps[:], EPS)
        unread_rstd = held.tile([P, 1], F32)
        nc.scalar.activation(unread_rstd[:], eps[:], Act.Abs_reciprocal_sqrt, bias=eps[:])

        base_tile = held.tile([P, WINDOWS, TOKENS], BF16)
        base_blocks = base.rearrange("(a p) i -> p a i", p=P)
        for a in range(0, WINDOWS, 2):
            nc.sync.dma_start(base_tile[:, a : a + 2, :], base_blocks[:, a : a + 2, :])
        offsets = held.tile([P, LIST // 16], U16)
        nc.sync.dma_start(offsets[:], offs)
        x_tile = held.tile([P, BLOCKS, LIST], BF16)
        w_tile = held.tile([P, BLOCKS, FEATURES], BF16)
        x_blocks = x.rearrange("(p k) j -> p k j", p=P)
        w_blocks = w.flatten_outer_dims().rearrange("(p k) m -> p k m", p=P)
        nc.sync.dma_start(x_tile[:, 0:2, :], x_blocks[:, 0:2, :])
        nc.sync.dma_start(w_tile[:, 0:1, :], w_blocks[:, 0:1, :])
        nc.sync.dma_start(w_tile[:, 1:2, :], w_blocks[:, 1:2, :])
        nc.sync.dma_start(x_tile[:, 2:4, :], x_blocks[:, 2:4, :])
        nc.sync.dma_start(w_tile[:, 2:4, :], w_blocks[:, 2:4, :])
        gain = held.tile([P, WINDOWS], F32)
        nc.sync.dma_start(gain[:], s.rearrange("(a p) o -> p (a o)", p=P))

        ident = held.tile([P, P], BF16)
        make_identity(nc, ident[:])
        mean_weights = held.tile([P, P], BF16)
        nc.vector.memset(mean_weights[:], 1.0 / FEATURES)

        windows = [psum.tile([P, TOKENS], F32, name=f"window{a}") for a in range(WINDOWS)]
        for a in range(WINDOWS):
            nc.tensor.matmul(windows[a][:], ident[:], base_tile[:, a, :], start=True, stop=False)

        for blocks in ((0,), (1,), (2, 3)):
            for a in range(WINDOWS):
                for k in blocks:
                    nc.tensor.matmul(
                        windows[a][:].indirect(offsets[:]),
                        w_tile[:, k, a * P : (a + 1) * P],
                        x_tile[:, k, :],
                        start=False,
                        stop=k == BLOCKS - 1,
                    )

        halves = [slice(h * HALF, (h + 1) * HALF) for h in range(2)]
        squared = [squares.tile([P, TOKENS], BF16, name="squared") for a in range(WINDOWS)]
        for a in range(WINDOWS - 1):
            nc.scalar.activation(squared[a][:], windows[a][:], Act.Square)
        for half in halves:
            nc.scalar.activation(squared[-1][:, half], windows[-1][:, half], Act.Square)
        means = [psum.tile([P, HALF], F32, name=f"mean{h}") for h in range(2)]
        for h in range(2):
            for a in range(WINDOWS):
                nc.tensor.matmul(
                    means[h][:], mean_weights[:], squared[a][:, halves[h]], start=a == 0, stop=a == WINDOWS - 1
                )

        for h in range(2):
            rstd = results.tile([P, HALF], F32)
            nc.scalar.activation(rstd[:], means[h][:], Act.Abs_reciprocal_sqrt, bias=eps[:])
            for a in range(WINDOWS):
                result = results.tile([P, HALF], F32)
                nc.vector.scalar_tensor_tensor(
                    result[:], windows[a][:, halves[h]], gain[:, a : a + 1], rstd[:], mult, mult
                )
                nc.sync.dma_start(out[a * P : (a + 1) * P, halves[h]], result[:])
